import numpy as np
import ml_dtypes


def mxq(x, axis, fmt="e4m3"):
    dtype, down = {"e4m3": (ml_dtypes.float8_e4m3fn, 7), "e5m2": (ml_dtypes.float8_e5m2, 14)}[fmt]
    v = np.moveaxis(np.asarray(x, np.float32).astype(ml_dtypes.bfloat16).astype(np.float64), axis, -1)
    blocks = v.reshape(v.shape[:-1] + (-1, 32))
    amax = np.abs(blocks).max(-1, keepdims=True)
    byte = np.maximum(np.where(amax > 0, np.frexp(amax)[1] - 1 + 127, 0) - down, 1)
    scale = np.exp2(byte - 127.0)
    codes = (blocks / scale).astype(np.float32).astype(dtype).astype(np.float64)
    return np.moveaxis((codes * scale).reshape(v.shape), -1, axis)


WIDE = False


def mx_kscale(k):
    if not WIDE:
        return np.ones(k)
    levels = np.array([10, -10, 5, -5, 0])
    if k % 512:
        return np.exp2(np.random.permutation(np.resize(levels, k // 32))).repeat(32)
    a = np.empty((k // 512, 16))
    for p in range(k // 512):
        a[p, :8] = np.random.permutation(np.resize(levels, 8))
        for g in range(8):
            far = levels[np.abs(levels - a[p, g]) >= 10]
            a[p, g + 8] = far[np.random.randint(len(far))]
    return np.exp2(a.ravel()).repeat(32)


def f64(x):
    return np.asarray(x).astype(np.float64)


def striped(idx):
    return np.tile(np.asarray(idx).reshape(-1, 16).T, (8, 1)).astype(np.uint16)


def unstriped(offs):
    return offs[:16].T.reshape(-1).astype(np.int64)


E2M1 = np.array([0.0, 0.5, 1.0, 1.5, 2.0, 3.0, 4.0, 6.0, -0.0, -0.5, -1.0, -1.5, -2.0, -3.0, -4.0, -6.0])


def pack_weight(w, fmt):
    k, n = w.shape
    w = f64(np.asarray(w, np.float32).astype(ml_dtypes.bfloat16)).reshape(k // 32, 32, n)
    amax = np.abs(w).max(1)
    if fmt == "e4m3":
        byte = np.frexp(amax)[1] - 1 + 127 - 7
    else:
        mant, ex = np.frexp(amax / 6.0)
        byte = np.where(mant > 0.5, ex, ex - 1) + 127
    byte = np.clip(np.where(amax > 0, byte, 1), 1, 254)
    scaled = (w * np.exp2(127.0 - byte)[:, None, :]).reshape(k, n).astype(np.float32)
    by_word = np.ascontiguousarray(scaled.reshape(k // 512, 128, 4, n).transpose(0, 1, 3, 2))
    if fmt == "e4m3":
        words = by_word.astype(ml_dtypes.float8_e4m3fn).view(np.uint8)
    else:
        c = by_word.astype(ml_dtypes.float4_e2m1fn).view(np.uint8) & 0xF
        words = (c[..., 0::2] | (c[..., 1::2] << 4)).reshape(k // 512, 128, 2 * n)
    return np.ascontiguousarray(words), np.ascontiguousarray(byte.astype(np.uint8).reshape(k // 512, 16, n))


def unpack_weight(words, scales, fmt):
    g, _, n = scales.shape
    words = np.ascontiguousarray(words).reshape(g, 128, n, -1)
    if fmt == "e4m3":
        vals = words.view(ml_dtypes.float8_e4m3fn).astype(np.float64)
    else:
        nib = np.empty((g, 128, n, 4), np.uint8)
        nib[..., 0::2] = words & 0xF
        nib[..., 1::2] = words >> 4
        vals = E2M1[nib]
    vals = vals * np.repeat(np.exp2(scales.astype(np.float64) - 127.0), 8, axis=1)[..., None]
    return vals.transpose(0, 1, 3, 2).reshape(g * 512, n)


def bf(x):
    return np.asarray(x, np.float32).astype(ml_dtypes.bfloat16)


def planes(Y):
    r, m = Y.shape
    b = f64(bf(Y)).reshape(r // 32, 32, m)
    amax = np.abs(b).max(1)
    byte = np.clip(np.where(amax > 0, np.frexp(amax)[1] - 1 + 127 - 7, 1), 1, 254)
    codes = (b * np.exp2(127.0 - byte)[:, None, :]).reshape(r, m).astype(np.float32).astype(ml_dtypes.float8_e4m3fn).view(np.uint8)
    words = codes.reshape(r // 512, 128, 4, m).transpose(0, 1, 3, 2)
    return np.ascontiguousarray(words), np.ascontiguousarray(byte.astype(np.uint8).reshape(r // 512, 16, m))


D, T, I, Q, E, U, X = 512, 2048, 512, 256, 512, 1024, 1024


def setup_inputs():
    n = np.random.standard_normal
    idx = np.random.permutation(T)[:I]
    idx2 = np.random.permutation(U)[:I]
    idx3 = np.random.permutation(X)[:I]
    fd = mx_kscale(D)
    fi = mx_kscale(I)
    keysp = pack_weight(n((D, T)) / fd[:, None], "e2m1")
    return {
        "query": (n((D, Q)) * 0.7 / np.sqrt(D) * fd[:, None]).astype(np.float32),
        "query2": (n((D, Q)) * 0.7 / np.sqrt(D) * fd[:, None]).astype(np.float32),
        "keys_words": keysp[0],
        "keys_scales": keysp[1],
        "notes": (n((D, U)) / fd[:, None]).astype(np.float32),
        "os": (np.random.uniform(0.02, 0.08, (1, I)) * fi).astype(np.float32),
        "vals": (n((E, T))).astype(np.float32),
        "vals2": (n((E, X))).astype(np.float32),
        "vsc": (np.random.uniform(0.5, 2.0, (1, I)) / fi).astype(np.float32),
        "offs": striped(idx),
        "offs2": striped(idx2),
        "offs3": striped(idx3),
    }


def reference(query, query2, keys_words, keys_scales, notes, os, vals, vals2, vsc, offs, offs2, offs3):
    idx = unstriped(offs)
    idx2 = unstriped(offs2)
    idx3 = unstriped(offs3)
    keysu = unpack_weight(keys_words, keys_scales, "e2m1")
    queryq = mxq(f64(query), 0, "e4m3")
    keysidxg = keysu[:, idx]
    query2q = mxq(f64(query2), 0, "e4m3")
    notesidx2q = mxq(f64(notes)[:, idx2], 0, "e4m3")
    w = queryq.T @ keysidxg + query2q.T @ notesidx2q
    wo1 = w * f64(os)
    wt1 = wo1.T
    vz = np.abs(f64(vals)[:, idx] - f64(vals2)[:, idx3]) * f64(vsc)
    vt1 = vz.T
    vt1q = mxq(vt1, 0, "e4m3")
    wt1q = mxq(wt1, 0, "e4m3")
    o = vt1q.T @ wt1q
    words, scales = planes(o)
    return o, words, scales

@@ -1,0 +1,216 @@
+from contextlib import ExitStack
+
+import concourse.mybir as mybir
+from concourse.masks import make_identity
+
+D, T, I, Q, E, U, X = 512, 2048, 512, 256, 512, 1024, 1024
+FLOPS = 2 * (2 * D * Q * I + I * E * Q)
+
+F32 = mybir.dt.float32
+BF16 = mybir.dt.bfloat16
+I32 = mybir.dt.int32
+U32 = mybir.dt.uint32
+U16 = mybir.dt.uint16
+U8 = mybir.dt.uint8
+FP8X4 = mybir.dt.float8_e4m3fn_x4
+FP4X4 = mybir.dt.float4_e2m1fn_x4
+COPY = mybir.ActivationFunctionType.Copy
+ABS = mybir.ActivationFunctionType.Abs
+MULT = mybir.AluOpType.mult
+SUB = mybir.AluOpType.subtract
+
+P = 128
+PACK = 4
+HALVES = Q // P
+
+
+def tile_attend_twosources_apartvalues_lean_pl_kernel(
+    tc, query, query2, keys_words, keys_scales, notes, wfac, vals, vals2, vfac, offs, offs2, offs3, out_0, out_1, out_2
+):
+    nc = tc.nc
+    with ExitStack() as ctx:
+        sb = ctx.enter_context(tc.tile_pool(name="sb", bufs=1))
+        ps = ctx.enter_context(tc.psum_pool(name="ps", bufs=1))
+        ps2 = ctx.enter_context(tc.psum_pool(name="ps2", bufs=2))
+
+        def tile(name, shape, dtype):
+            return sb.tile(shape, dtype, name=name, align_bytes=64)
+
+        def planes(name, width):
+            return [tile("%s%d" % (name, j), [P, width], F32) for j in range(PACK)]
+
+        tok_list = tile("tok_list", [P, I // 16], U16)
+        note_list = tile("note_list", [P, I // 16], U16)
+        col_list = tile("col_list", [P, I // 16], U16)
+        key_pool = tile("key_pool", [P, T], U16)
+        key_scale_pool = tile("key_scale_pool", [P, T], U8)
+        note_pool = planes("note_pool", U)
+        val_pool = planes("val_pool", T)
+        val2_pool = [tile("val2_pool%d" % u, [P, 2 * X], F32) for u in range(2)]
+        q_raw = [tile("q_raw%d" % a, [P, PACK, Q], F32) for a in range(2)]
+        wfac_sb = tile("wfac_sb", [P, PACK], F32)
+        vfac_sb = tile("vfac_sb", [P, PACK], F32)
+        ident = tile("ident", [P, P], F32)
+
+        notes_v = notes.rearrange("(p j) u -> p j u", j=PACK)
+        vals_v = vals.rearrange("(p j) u -> p j u", j=PACK)
+        vals2_v = vals2.rearrange("(p j) u -> p j u", j=PACK)
+
+        nc.gpsimd.memset(key_scale_pool[:].bitcast(I32), 0)
+        make_identity(nc, ident[:])
+
+        nc.sync.dma_start(key_pool[:].bitcast(I32), keys_words[0].bitcast(I32))
+        nc.sync.dma_start(tok_list[:], offs)
+        nc.sync.dma_start(note_pool[0][:], notes_v[:, 0, :])
+        nc.sync.dma_start(note_list[:], offs2)
+        nc.sync.dma_start(note_pool[1][:], notes_v[:, 1, :])
+        nc.sync.dma_start(q_raw[0][:], query.rearrange("(p j) q -> p j q", j=PACK))
+        nc.sync.dma_start(note_pool[2][:], notes_v[:, 2, :])
+        nc.sync.dma_start(note_pool[3][:], notes_v[:, 3, :])
+        for g in range(4):
+            nc.sync.dma_start(
+                out=key_scale_pool[32 * g : 32 * g + 4, :].bitcast(I32),
+                in_=keys_scales[0, 4 * g : 4 * g + 4, :].bitcast(I32),
+            )
+        nc.sync.dma_start(q_raw[1][:], query2.rearrange("(p j) q -> p j q", j=PACK))
+        nc.sync.dma_start(out=wfac_sb[:], in_=wfac.rearrange("o (p r) -> (o p) r", r=PACK))
+        for j in range(PACK):
+            if j % 2 == 0:
+                nc.sync.dma_start(val2_pool[j // 2][:], vals2_v[:, j : j + 2, :].rearrange("p j x -> p (j x)"))
+            if j == 0:
+                nc.sync.dma_start(col_list[:], offs3)
+                nc.sync.dma_start(out=vfac_sb[:], in_=vfac.rearrange("o (p r) -> (o p) r", r=PACK))
+            nc.sync.dma_start(val_pool[j][:], vals_v[:, j, :])
+
+        key_listed = tile("key_listed", [P, I], U16)
+        key_words = tile("key_words", [P, PACK, P], U16)
+        key_scale = tile("key_scale", [P, PACK, P], U8)
+        nc.vector.tensor_copy(key_listed[:], key_pool[:].indirect(tok_list[:]))
+        nc.vector.tensor_copy(key_words[:], key_listed[:].rearrange("p (s r) -> p r s", r=PACK))
+
+        def quantise_queries(a, round_and_weave):
+            q_bf = tile("q_bf%d" % a, [P, Q, PACK], BF16)
+            round_and_weave(q_bf[:], q_raw[a][:].rearrange("p j q -> p q j"))
+            words = tile("q_words%d" % a, [P, Q], U32)
+            scale = tile("q_scale%d" % a, [P, Q], U8)
+            nc.vector.quantize_mx(out=words[:].bitcast(FP8X4), scales=scale[:], in_=q_bf[:].rearrange("p q j -> p (q j)"))
+            return words, scale
+
+        note_listed = tile("note_listed", [P, PACK, I], BF16)
+        for j in range(PACK):
+            nc.scalar.activation(note_listed[:, j, :], note_pool[j][:].indirect(note_list[:]), COPY)
+        q_key = quantise_queries(0, nc.vector.tensor_copy)
+        nc.vector.tensor_copy(key_scale[:].rearrange("p r s -> p s r"), key_scale_pool[:].indirect(tok_list[:]))
+        note_bf = tile("note_bf", [P, PACK, P, PACK], BF16)
+        nc.vector.tensor_copy(note_bf[:], note_listed[:].rearrange("p j (s r) -> p r s j", r=PACK))
+        note_words = tile("note_words", [P, I], U32)
+        note_scale = tile("note_scale", [P, I], U8)
+        nc.vector.quantize_mx(
+            out=note_words[:].bitcast(FP8X4), scales=note_scale[:], in_=note_bf[:].rearrange("p r s j -> p (r s j)")
+        )
+        q_note = quantise_queries(1, nc.scalar.copy)
+        q_words, q_scale = zip(q_key, q_note)
+
+        w_words, w_scale = [], []
+        for h in range(HALVES):
+            cols = slice(h * P, (h + 1) * P)
+            score = ps.tile([P, PACK, P], F32, name="score%d" % h)
+            for r in range(PACK):
+                nc.tensor.matmul_mx(
+                    out=score[:, r, :],
+                    lhsT=key_words[:, r, :].bitcast(FP4X4),
+                    lhsT_scale=key_scale[:, r, :],
+                    rhs=q_words[0][:, cols].bitcast(FP8X4),
+                    rhs_scale=q_scale[0][:, cols],
+                    start=True,
+                    stop=False,
+                )
+                nc.tensor.matmul_mx(
+                    out=score[:, r, :],
+                    lhsT=note_words[:, r * P : (r + 1) * P].bitcast(FP8X4),
+                    lhsT_scale=note_scale[:, r * P : (r + 1) * P],
+                    rhs=q_words[1][:, cols].bitcast(FP8X4),
+                    rhs_scale=q_scale[1][:, cols],
+                    start=False,
+                    stop=True,
+                )
+            w_bf = tile("w_bf%d" % h, [P, P, PACK], BF16)
+            nc.vector.tensor_tensor(
+                w_bf[:], score[:].rearrange("s r q -> s q r"), wfac_sb[:].unsqueeze(1).to_broadcast([P, P, PACK]), MULT
+            )
+            w_words.append(tile("w_words%d" % h, [P, P], U32))
+            w_scale.append(tile("w_scale%d" % h, [P, P], U8))
+            nc.vector.quantize_mx(
+                out=w_words[h][:].bitcast(FP8X4), scales=w_scale[h][:], in_=w_bf[:].rearrange("s q r -> s (q r)")
+            )
+
+        res_bank = [ps.tile([P, PACK, P], F32, name="res_bank%d" % h) for h in range(HALVES)]
+        res = tile("res", [P, PACK, Q], F32)
+        out_v = out_0.rearrange("(p j) q -> p j q", j=PACK)
+        last = PACK - 1
+
+        def turn(j, second):
+            diff = sb.tile([P, I], F32, name="diff%d" % j, tag="second2" if j == 1 else "diff%d" % j, align_bytes=64)
+            nc.vector.tensor_tensor(diff[:], val_pool[j][:].indirect(tok_list[:]), second, SUB)
+            dist = tile("dist%d" % j, [P, PACK, P], F32)
+            nc.scalar.activation(dist[:].rearrange("p r s -> p s r"), diff[:].rearrange("p (s r) -> p s r", r=PACK), ABS)
+            turned = ps2.tile([P, PACK, P], F32, name="turned")
+            for r in range(PACK):
+                nc.tensor.transpose(turned[:, r, :], dist[:, r, :], ident[:])
+            return turned
+
+        def multiply(j, turned):
+            v_bf = sb.tile([P, P, PACK], BF16, name="v_bf%d" % j, tag="second%d" % (j + 1) if j % 2 == 0 else "v_bf%d" % j, align_bytes=64)
+            nc.vector.tensor_tensor(
+                v_bf[:], turned[:].rearrange("s r p -> s p r"), vfac_sb[:].unsqueeze(1).to_broadcast([P, P, PACK]), MULT
+            )
+            v_words = tile("v_words%d" % j, [P, P], U32)
+            v_scale = tile("v_scale%d" % j, [P, P], U8)
+            nc.vector.quantize_mx(
+                out=v_words[:].bitcast(FP8X4), scales=v_scale[:], in_=v_bf[:].rearrange("s p r -> s (p r)")
+            )
+            for h in range(HALVES):
+                nc.tensor.matmul_mx(
+                    out=res_bank[h][:, j, :],
+                    lhsT=v_words[:].bitcast(FP8X4),
+                    lhsT_scale=v_scale[:],
+                    rhs=w_words[h][:].bitcast(FP8X4),
+                    rhs_scale=w_scale[h][:],
+                    start=True,
+                    stop=True,
+                )
+            if j < last:
+                for h in range(HALVES):
+                    nc.scalar.copy(res[:, j, h * P : (h + 1) * P], res_bank[h][:, j, :])
+
+        for u in range(2):
+            second = []
+            for c in range(2):
+                j = 2 * u + c
+                second.append(sb.tile([P, I], F32, name="second%d" % j, tag="second%d" % j, align_bytes=64))
+                window = val2_pool[u][:, c * X : (c + 1) * X]
+                nc.scalar.activation(second[c][:], window.indirect(col_list[:]), COPY)
+            banks = [turn(2 * u + c, second[c][:]) for c in range(2)]
+            for c in range(2):
+                multiply(2 * u + c, banks[c])
+        nc.sync.dma_start(out=out_v[:, : PACK - 1, :], in_=res[:, : PACK - 1, :])
+
+        res_bf = tile("res_bf", [P, Q, PACK], BF16)
+        nc.vector.tensor_copy(res_bf[:, :P, :], res_bank[0][:].rearrange("p j q -> p q j"))
+        nc.scalar.copy(res_bf[:, P:, :], res_bank[1][:].rearrange("p j q -> p q j"))
+        for h in reversed(range(HALVES)):
+            nc.scalar.copy(res[:, last, h * P : (h + 1) * P], res_bank[h][:, last, :])
+        res_words = tile("res_words", [P, Q], U32)
+        res_scale = tile("res_scale", [P, Q], U8)
+        nc.vector.quantize_mx(
+            out=res_words[:].bitcast(FP8X4), scales=res_scale[:], in_=res_bf[:].rearrange("p q j -> p (q j)")
+        )
+        nc.scalar.dma_start(out=out_v[:, last, :], in_=res[:, last, :])
+        nc.sync.dma_start(
+            out=out_1[0].rearrange("p q j -> p (q j)").bitcast(I32), in_=res_words[:].bitcast(I32)
+        )
+        for g in range(4):
+            queue = nc.sync if g % 2 == 0 else nc.scalar
+            queue.dma_start(
+                out=out_2[0, 4 * g : 4 * g + 4, :].bitcast(I32), in_=res_scale[32 * g : 32 * g + 4, :].bitcast(I32)
+            )

@@ -59,19 +59,24 @@ def tile_attend_twosources_apartvalues_lean_pl_kernel(
         nc.gpsimd.memset(key_scale_pool[:].bitcast(I32), 0)
         make_identity(nc, ident[:])
 
-        nc.sync.dma_start(key_pool[:].bitcast(I32), keys_words[0].bitcast(I32))
-        nc.sync.dma_start(tok_list[:], offs)
-        nc.sync.dma_start(note_pool[0][:], notes_v[:, 0, :])
-        nc.sync.dma_start(note_list[:], offs2)
-        nc.sync.dma_start(note_pool[1][:], notes_v[:, 1, :])
-        nc.sync.dma_start(q_raw[0][:], query.rearrange("(p j) q -> p j q", j=PACK))
-        nc.sync.dma_start(note_pool[2][:], notes_v[:, 2, :])
-        nc.sync.dma_start(note_pool[3][:], notes_v[:, 3, :])
-        for g in range(4):
+        def load_key_scales(g):
             nc.sync.dma_start(
                 out=key_scale_pool[32 * g : 32 * g + 4, :].bitcast(I32),
                 in_=keys_scales[0, 4 * g : 4 * g + 4, :].bitcast(I32),
             )
+
+        nc.sync.dma_start(key_pool[:].bitcast(I32), keys_words[0].bitcast(I32))
+        nc.sync.dma_start(tok_list[:], offs)
+        load_key_scales(0)
+        nc.sync.dma_start(note_pool[0][:], notes_v[:, 0, :])
+        load_key_scales(1)
+        nc.sync.dma_start(note_list[:], offs2)
+        nc.sync.dma_start(note_pool[1][:], notes_v[:, 1, :])
+        load_key_scales(2)
+        nc.sync.dma_start(q_raw[0][:], query.rearrange("(p j) q -> p j q", j=PACK))
+        load_key_scales(3)
+        nc.sync.dma_start(note_pool[2][:], notes_v[:, 2, :])
+        nc.sync.dma_start(note_pool[3][:], notes_v[:, 3, :])
         nc.sync.dma_start(q_raw[1][:], query2.rearrange("(p j) q -> p j q", j=PACK))
         nc.sync.dma_start(out=wfac_sb[:], in_=wfac.rearrange("o (p r) -> (o p) r", r=PACK))
         for j in range(PACK):
@@ -112,31 +117,34 @@ def tile_attend_twosources_apartvalues_lean_pl_kernel(
         q_words, q_scale = zip(q_key, q_note)
 
         w_words, w_scale = [], []
+        score = [ps.tile([P, PACK, P], F32, name="score%d" % h) for h in range(HALVES)]
         for h in range(HALVES):
             cols = slice(h * P, (h + 1) * P)
-            score = ps.tile([P, PACK, P], F32, name="score%d" % h)
             for r in range(PACK):
                 nc.tensor.matmul_mx(
-                    out=score[:, r, :],
+                    out=score[h][:, r, :],
                     lhsT=key_words[:, r, :].bitcast(FP4X4),
                     lhsT_scale=key_scale[:, r, :],
                     rhs=q_words[0][:, cols].bitcast(FP8X4),
                     rhs_scale=q_scale[0][:, cols],
-                    start=True,
+                    start=(r == 0),
                     stop=False,
                 )
+        for h in range(HALVES):
+            cols = slice(h * P, (h + 1) * P)
+            for r in range(PACK):
                 nc.tensor.matmul_mx(
-                    out=score[:, r, :],
+                    out=score[h][:, r, :],
                     lhsT=note_words[:, r * P : (r + 1) * P].bitcast(FP8X4),
                     lhsT_scale=note_scale[:, r * P : (r + 1) * P],
                     rhs=q_words[1][:, cols].bitcast(FP8X4),
                     rhs_scale=q_scale[1][:, cols],
                     start=False,
-                    stop=True,
+                    stop=(r == PACK - 1),
                 )
             w_bf = tile("w_bf%d" % h, [P, P, PACK], BF16)
             nc.vector.tensor_tensor(
-                w_bf[:], score[:].rearrange("s r q -> s q r"), wfac_sb[:].unsqueeze(1).to_broadcast([P, P, PACK]), MULT
+                w_bf[:], score[h][:].rearrange("s r q -> s q r"), wfac_sb[:].unsqueeze(1).to_broadcast([P, P, PACK]), MULT
             )
             w_words.append(tile("w_words%d" % h, [P, P], U32))
             w_scale.append(tile("w_scale%d" % h, [P, P], U8))
@@ -145,15 +153,24 @@ def tile_attend_twosources_apartvalues_lean_pl_kernel(
             )
 
         res_bank = [ps.tile([P, PACK, P], F32, name="res_bank%d" % h) for h in range(HALVES)]
-        res = tile("res", [P, PACK, Q], F32)
+        res = sb.tile([P, PACK, Q], F32, name="res", tag="val2_pool1", align_bytes=64)
         out_v = out_0.rearrange("(p j) q -> p j q", j=PACK)
         last = PACK - 1
 
         def turn(j, second):
-            diff = sb.tile([P, I], F32, name="diff%d" % j, tag="second2" if j == 1 else "diff%d" % j, align_bytes=64)
-            nc.vector.tensor_tensor(diff[:], val_pool[j][:].indirect(tok_list[:]), second, SUB)
+            diff = sb.tile([P, I], F32, name="diff%d" % j, tag="diff%d" % j, align_bytes=64)
             dist = tile("dist%d" % j, [P, PACK, P], F32)
-            nc.scalar.activation(dist[:].rearrange("p r s -> p s r"), diff[:].rearrange("p (s r) -> p s r", r=PACK), ABS)
+            pieces = 2 if j == last else 1
+            for c in range(pieces):
+                n = I // pieces
+                slots = slice(c * n, (c + 1) * n)
+                listed = val_pool[j][:].indirect(tok_list[:, c * n // 16 : (c + 1) * n // 16])
+                nc.vector.tensor_tensor(diff[:, slots], listed, second[:, slots], SUB)
+                nc.scalar.activation(
+                    dist[:, :, c * n // PACK : (c + 1) * n // PACK].rearrange("p r s -> p s r"),
+                    diff[:, slots].rearrange("p (s r) -> p s r", r=PACK),
+                    ABS,
+                )
             turned = ps2.tile([P, PACK, P], F32, name="turned")
             for r in range(PACK):
                 nc.tensor.transpose(turned[:, r, :], dist[:, r, :], ident[:])
@@ -182,6 +199,10 @@ def tile_attend_twosources_apartvalues_lean_pl_kernel(
             if j < last:
                 for h in range(HALVES):
                     nc.scalar.copy(res[:, j, h * P : (h + 1) * P], res_bank[h][:, j, :])
+            if j == 1:
+                nc.sync.dma_start(out=out_v[:, :2, :], in_=res[:, :2, :])
+            if j == 2:
+                nc.sync.dma_start(out=out_v[:, 2, :], in_=res[:, 2, :])
 
         for u in range(2):
             second = []
@@ -190,10 +211,9 @@ def tile_attend_twosources_apartvalues_lean_pl_kernel(
                 second.append(sb.tile([P, I], F32, name="second%d" % j, tag="second%d" % j, align_bytes=64))
                 window = val2_pool[u][:, c * X : (c + 1) * X]
                 nc.scalar.activation(second[c][:], window.indirect(col_list[:]), COPY)
-            banks = [turn(2 * u + c, second[c][:]) for c in range(2)]
+            banks = [turn(2 * u + c, second[c]) for c in range(2)]
             for c in range(2):
                 multiply(2 * u + c, banks[c])
-        nc.sync.dma_start(out=out_v[:, : PACK - 1, :], in_=res[:, : PACK - 1, :])
 
         res_bf = tile("res_bf", [P, Q, PACK], BF16)
         nc.vector.tensor_copy(res_bf[:, :P, :], res_bank[0][:].rearrange("p j q -> p q j"))

@@ -21,7 +21,14 @@ SUB = mybir.AluOpType.subtract
 
 P = 128
 PACK = 4
+LAST = PACK - 1
 HALVES = Q // P
+GROUP = 16
+QUADRANTS, QUADRANT = 4, 32
+SCALE_ROWS = 4
+BLOCK_PARTITIONS = 8
+LINE_F32, LINE_WORDS = 4, 2
+TAIL_PIECES = 2
 
 
 def tile_attend_twosources_apartvalues_lean_pl_kernel(
@@ -31,17 +38,26 @@ def tile_attend_twosources_apartvalues_lean_pl_kernel(
     with ExitStack() as ctx:
         sb = ctx.enter_context(tc.tile_pool(name="sb", bufs=1))
         ps = ctx.enter_context(tc.psum_pool(name="ps", bufs=1))
-        ps2 = ctx.enter_context(tc.psum_pool(name="ps2", bufs=2))
+        ps_turned = ctx.enter_context(tc.psum_pool(name="ps_turned", bufs=2))
 
-        def tile(name, shape, dtype):
-            return sb.tile(shape, dtype, name=name, align_bytes=64)
+        def tile(name, shape, dtype, after=None):
+            return sb.tile(shape, dtype, name=name, tag=after or name, align_bytes=64)
 
         def planes(name, width):
-            return [tile("%s%d" % (name, j), [P, width], F32) for j in range(PACK)]
+            return [tile("%s%d" % (name, t), [P, width], F32) for t in range(PACK)]
 
-        tok_list = tile("tok_list", [P, I // 16], U16)
-        note_list = tile("note_list", [P, I // 16], U16)
-        col_list = tile("col_list", [P, I // 16], U16)
+        def by_plane(rows):
+            return rows.rearrange("(p t) c -> p t c", t=PACK)
+
+        def by_slot(factors):
+            return factors.rearrange("o (s r) -> (o s) r", r=PACK)
+
+        def scale_rows(scales, g):
+            return scales[QUADRANT * g : QUADRANT * g + SCALE_ROWS]
+
+        tok_list = tile("tok_list", [P, I // GROUP], U16)
+        note_list = tile("note_list", [P, I // GROUP], U16)
+        col_list = tile("col_list", [P, I // GROUP], U16)
         key_pool = tile("key_pool", [P, T], U16)
         key_scale_pool = tile("key_scale_pool", [P, T], U8)
         note_pool = planes("note_pool", U)
@@ -52,185 +68,177 @@ def tile_attend_twosources_apartvalues_lean_pl_kernel(
         vfac_sb = tile("vfac_sb", [P, PACK], F32)
         ident = tile("ident", [P, P], F32)
 
-        notes_v = notes.rearrange("(p j) u -> p j u", j=PACK)
-        vals_v = vals.rearrange("(p j) u -> p j u", j=PACK)
-        vals2_v = vals2.rearrange("(p j) u -> p j u", j=PACK)
-
         nc.gpsimd.memset(key_scale_pool[:].bitcast(I32), 0)
         make_identity(nc, ident[:])
 
-        def load_key_scales(g):
-            nc.sync.dma_start(
-                out=key_scale_pool[32 * g : 32 * g + 4, :].bitcast(I32),
-                in_=keys_scales[0, 4 * g : 4 * g + 4, :].bitcast(I32),
-            )
-
         nc.sync.dma_start(key_pool[:].bitcast(I32), keys_words[0].bitcast(I32))
         nc.sync.dma_start(tok_list[:], offs)
-        load_key_scales(0)
-        nc.sync.dma_start(note_pool[0][:], notes_v[:, 0, :])
-        load_key_scales(1)
+        nc.sync.dma_start(key_scale_pool[0:P:BLOCK_PARTITIONS, :].bitcast(I32), keys_scales[0].bitcast(I32))
+        nc.sync.dma_start(note_pool[0][:], by_plane(notes)[:, 0, :])
         nc.sync.dma_start(note_list[:], offs2)
-        nc.sync.dma_start(note_pool[1][:], notes_v[:, 1, :])
-        load_key_scales(2)
-        nc.sync.dma_start(q_raw[0][:], query.rearrange("(p j) q -> p j q", j=PACK))
-        load_key_scales(3)
-        nc.sync.dma_start(note_pool[2][:], notes_v[:, 2, :])
-        nc.sync.dma_start(note_pool[3][:], notes_v[:, 3, :])
-        nc.sync.dma_start(q_raw[1][:], query2.rearrange("(p j) q -> p j q", j=PACK))
-        nc.sync.dma_start(out=wfac_sb[:], in_=wfac.rearrange("o (p r) -> (o p) r", r=PACK))
-        for j in range(PACK):
-            if j % 2 == 0:
-                nc.sync.dma_start(val2_pool[j // 2][:], vals2_v[:, j : j + 2, :].rearrange("p j x -> p (j x)"))
-            if j == 0:
-                nc.sync.dma_start(col_list[:], offs3)
-                nc.sync.dma_start(out=vfac_sb[:], in_=vfac.rearrange("o (p r) -> (o p) r", r=PACK))
-            nc.sync.dma_start(val_pool[j][:], vals_v[:, j, :])
+        nc.sync.dma_start(note_pool[1][:], by_plane(notes)[:, 1, :])
+        nc.sync.dma_start(q_raw[0][:], by_plane(query))
+        nc.sync.dma_start(note_pool[2][:], by_plane(notes)[:, 2, :])
+        nc.sync.dma_start(note_pool[3][:], by_plane(notes)[:, 3, :])
+        nc.sync.dma_start(q_raw[1][:], by_plane(query2))
 
         key_listed = tile("key_listed", [P, I], U16)
         key_words = tile("key_words", [P, PACK, P], U16)
         key_scale = tile("key_scale", [P, PACK, P], U8)
         nc.vector.tensor_copy(key_listed[:], key_pool[:].indirect(tok_list[:]))
         nc.vector.tensor_copy(key_words[:], key_listed[:].rearrange("p (s r) -> p r s", r=PACK))
+        key_scale_listed = tile("key_scale_listed", [P, PACK, P], U8)
+        nc.vector.tensor_copy(key_scale_listed[:].rearrange("p r s -> p s r"), key_scale_pool[:].indirect(tok_list[:]))
+        nc.gpsimd.memset(key_scale[:].rearrange("p r s -> p (r s)").bitcast(I32), 0)
+        for g in range(QUADRANTS):
+            spread = key_scale_listed[QUADRANT * g : QUADRANT * (g + 1) : BLOCK_PARTITIONS]
+            nc.sync.dma_start(
+                scale_rows(key_scale, g).rearrange("p r s -> p (r s)").bitcast(I32),
+                spread.rearrange("p r s -> p (r s)").bitcast(I32),
+            )
 
-        def quantise_queries(a, round_and_weave):
-            q_bf = tile("q_bf%d" % a, [P, Q, PACK], BF16)
-            round_and_weave(q_bf[:], q_raw[a][:].rearrange("p j q -> p q j"))
-            words = tile("q_words%d" % a, [P, Q], U32)
-            scale = tile("q_scale%d" % a, [P, Q], U8)
-            nc.vector.quantize_mx(out=words[:].bitcast(FP8X4), scales=scale[:], in_=q_bf[:].rearrange("p q j -> p (q j)"))
+        nc.sync.dma_start(wfac_sb[:], by_slot(wfac))
+        for t in range(PACK):
+            if t % 2 == 0:
+                nc.sync.dma_start(val2_pool[t // 2][:], by_plane(vals2)[:, t : t + 2, :].rearrange("p t x -> p (t x)"))
+            if t == 0:
+                nc.sync.dma_start(col_list[:], offs3)
+                nc.sync.dma_start(vfac_sb[:], by_slot(vfac))
+            nc.sync.dma_start(val_pool[t][:], by_plane(vals)[:, t, :])
+
+        def quantise(name, values, width, after=None):
+            words = tile(name + "_words", [P, width], U32, after=after)
+            scale = tile(name + "_scale", [P, width], U8)
+            nc.vector.quantize_mx(out=words[:].bitcast(FP8X4), scales=scale[:], in_=values)
             return words, scale
 
-        note_listed = tile("note_listed", [P, PACK, I], BF16)
-        for j in range(PACK):
-            nc.scalar.activation(note_listed[:, j, :], note_pool[j][:].indirect(note_list[:]), COPY)
-        q_key = quantise_queries(0, nc.vector.tensor_copy)
-        nc.vector.tensor_copy(key_scale[:].rearrange("p r s -> p s r"), key_scale_pool[:].indirect(tok_list[:]))
-        note_bf = tile("note_bf", [P, PACK, P, PACK], BF16)
-        nc.vector.tensor_copy(note_bf[:], note_listed[:].rearrange("p j (s r) -> p r s j", r=PACK))
-        note_words = tile("note_words", [P, I], U32)
-        note_scale = tile("note_scale", [P, I], U8)
-        nc.vector.quantize_mx(
-            out=note_words[:].bitcast(FP8X4), scales=note_scale[:], in_=note_bf[:].rearrange("p r s j -> p (r s j)")
-        )
-        q_note = quantise_queries(1, nc.scalar.copy)
-        q_words, q_scale = zip(q_key, q_note)
+        def weave_queries(a, copy):
+            q_bf = tile("q_bf%d" % a, [P, Q, PACK], BF16)
+            copy(
+                q_bf[:].rearrange("p (c n) t -> p c t n", n=LINE_F32),
+                q_raw[a][:].rearrange("p t (c n) -> p c t n", n=LINE_F32),
+            )
+            return q_bf[:].rearrange("p q t -> p (q t)")
 
-        w_words, w_scale = [], []
+        def factor(factors):
+            return factors[:].unsqueeze(1).to_broadcast([P, P, PACK])
+
+        q_key_words, q_key_scale = quantise("q_key", weave_queries(0, nc.vector.tensor_copy), Q)
+        note_listed = tile("note_listed", [P, PACK, I], BF16)
+        for t in range(PACK):
+            nc.scalar.activation(note_listed[:, t, :], note_pool[t][:].indirect(note_list[:]), COPY)
+        q_note_bf = weave_queries(1, nc.scalar.copy)
+        note_bf = tile("note_bf", [P, PACK, P, PACK], BF16)
+        nc.vector.tensor_copy(
+            note_bf[:].rearrange("p r (c n) t -> p r c t n", n=LINE_WORDS),
+            note_listed[:].rearrange("p t (c n r) -> p r c t n", n=LINE_WORDS, r=PACK),
+        )
+        q_note_words, q_note_scale = quantise("q_note", q_note_bf, Q)
+        note_words, note_scale = quantise("note", note_bf[:].rearrange("p r s t -> p (r s t)"), I)
+
         score = [ps.tile([P, PACK, P], F32, name="score%d" % h) for h in range(HALVES)]
         for h in range(HALVES):
-            cols = slice(h * P, (h + 1) * P)
+            rows = slice(h * P, (h + 1) * P)
             for r in range(PACK):
                 nc.tensor.matmul_mx(
                     out=score[h][:, r, :],
                     lhsT=key_words[:, r, :].bitcast(FP4X4),
                     lhsT_scale=key_scale[:, r, :],
-                    rhs=q_words[0][:, cols].bitcast(FP8X4),
-                    rhs_scale=q_scale[0][:, cols],
+                    rhs=q_key_words[:, rows].bitcast(FP8X4),
+                    rhs_scale=q_key_scale[:, rows],
                     start=(r == 0),
                     stop=False,
                 )
         for h in range(HALVES):
-            cols = slice(h * P, (h + 1) * P)
+            rows = slice(h * P, (h + 1) * P)
             for r in range(PACK):
                 nc.tensor.matmul_mx(
                     out=score[h][:, r, :],
                     lhsT=note_words[:, r * P : (r + 1) * P].bitcast(FP8X4),
                     lhsT_scale=note_scale[:, r * P : (r + 1) * P],
-                    rhs=q_words[1][:, cols].bitcast(FP8X4),
-                    rhs_scale=q_scale[1][:, cols],
+                    rhs=q_note_words[:, rows].bitcast(FP8X4),
+                    rhs_scale=q_note_scale[:, rows],
                     start=False,
-                    stop=(r == PACK - 1),
+                    stop=(r == LAST),
                 )
-            w_bf = tile("w_bf%d" % h, [P, P, PACK], BF16)
-            nc.vector.tensor_tensor(
-                w_bf[:], score[h][:].rearrange("s r q -> s q r"), wfac_sb[:].unsqueeze(1).to_broadcast([P, P, PACK]), MULT
-            )
-            w_words.append(tile("w_words%d" % h, [P, P], U32))
-            w_scale.append(tile("w_scale%d" % h, [P, P], U8))
-            nc.vector.quantize_mx(
-                out=w_words[h][:].bitcast(FP8X4), scales=w_scale[h][:], in_=w_bf[:].rearrange("s q r -> s (q r)")
-            )
 
         res_bank = [ps.tile([P, PACK, P], F32, name="res_bank%d" % h) for h in range(HALVES)]
-        res = sb.tile([P, PACK, Q], F32, name="res", tag="val2_pool1", align_bytes=64)
-        out_v = out_0.rearrange("(p j) q -> p j q", j=PACK)
-        last = PACK - 1
 
-        def turn(j, second):
-            diff = sb.tile([P, I], F32, name="diff%d" % j, tag="diff%d" % j, align_bytes=64)
-            dist = tile("dist%d" % j, [P, PACK, P], F32)
-            pieces = 2 if j == last else 1
+        def turn(t, second):
+            diff = tile("diff%d" % t, [P, I], F32)
+            dist = tile("dist%d" % t, [P, PACK, P], F32)
+            pieces = TAIL_PIECES if t == LAST else 1
+            n = I // pieces
             for c in range(pieces):
-                n = I // pieces
                 slots = slice(c * n, (c + 1) * n)
-                listed = val_pool[j][:].indirect(tok_list[:, c * n // 16 : (c + 1) * n // 16])
+                listed = val_pool[t][:].indirect(tok_list[:, c * n // GROUP : (c + 1) * n // GROUP])
                 nc.vector.tensor_tensor(diff[:, slots], listed, second[:, slots], SUB)
                 nc.scalar.activation(
                     dist[:, :, c * n // PACK : (c + 1) * n // PACK].rearrange("p r s -> p s r"),
                     diff[:, slots].rearrange("p (s r) -> p s r", r=PACK),
                     ABS,
                 )
-            turned = ps2.tile([P, PACK, P], F32, name="turned")
+            turned = ps_turned.tile([P, PACK, P], F32, name="turned")
             for r in range(PACK):
                 nc.tensor.transpose(turned[:, r, :], dist[:, r, :], ident[:])
             return turned
 
-        def multiply(j, turned):
-            v_bf = sb.tile([P, P, PACK], BF16, name="v_bf%d" % j, tag="second%d" % (j + 1) if j % 2 == 0 else "v_bf%d" % j, align_bytes=64)
-            nc.vector.tensor_tensor(
-                v_bf[:], turned[:].rearrange("s r p -> s p r"), vfac_sb[:].unsqueeze(1).to_broadcast([P, P, PACK]), MULT
-            )
-            v_words = tile("v_words%d" % j, [P, P], U32)
-            v_scale = tile("v_scale%d" % j, [P, P], U8)
-            nc.vector.quantize_mx(
-                out=v_words[:].bitcast(FP8X4), scales=v_scale[:], in_=v_bf[:].rearrange("s p r -> s (p r)")
-            )
+        def weigh_scores():
+            w_bf = tile("w_bf", [P, Q, PACK], BF16, after="second0")
+            for h in range(HALVES):
+                nc.vector.tensor_tensor(
+                    w_bf[:, h * P : (h + 1) * P, :], score[h][:].rearrange("s r q -> s q r"), factor(wfac_sb), MULT
+                )
+            return quantise("w", w_bf[:].rearrange("s q r -> s (q r)"), Q, after="val_pool1")
+
+        def multiply(t, turned, w_words, w_scale):
+            v_bf = tile("v_bf%d" % t, [P, P, PACK], BF16, after="second%d" % (t + 1) if t % 2 == 0 else None)
+            nc.vector.tensor_tensor(v_bf[:], turned[:].rearrange("s r p -> s p r"), factor(vfac_sb), MULT)
+            v_words, v_scale = quantise("v%d" % t, v_bf[:].rearrange("s p r -> s (p r)"), P)
             for h in range(HALVES):
                 nc.tensor.matmul_mx(
-                    out=res_bank[h][:, j, :],
+                    out=res_bank[h][:, t, :],
                     lhsT=v_words[:].bitcast(FP8X4),
                     lhsT_scale=v_scale[:],
-                    rhs=w_words[h][:].bitcast(FP8X4),
-                    rhs_scale=w_scale[h][:],
+                    rhs=w_words[:, h * P : (h + 1) * P].bitcast(FP8X4),
+                    rhs_scale=w_scale[:, h * P : (h + 1) * P],
                     start=True,
                     stop=True,
                 )
-            if j < last:
-                for h in range(HALVES):
-                    nc.scalar.copy(res[:, j, h * P : (h + 1) * P], res_bank[h][:, j, :])
-            if j == 1:
-                nc.sync.dma_start(out=out_v[:, :2, :], in_=res[:, :2, :])
-            if j == 2:
-                nc.sync.dma_start(out=out_v[:, 2, :], in_=res[:, 2, :])
 
-        for u in range(2):
+        def hand_out(res, done, queue):
+            for h in reversed(range(HALVES)):
+                nc.scalar.copy(res[:, done, h * P : (h + 1) * P], res_bank[h][:, done, :])
+            queue.dma_start(out=by_plane(out_0)[:, done, :], in_=res[:, done, :])
+
+        def gather_and_turn(pair):
             second = []
             for c in range(2):
-                j = 2 * u + c
-                second.append(sb.tile([P, I], F32, name="second%d" % j, tag="second%d" % j, align_bytes=64))
-                window = val2_pool[u][:, c * X : (c + 1) * X]
+                second.append(tile("second%d" % (2 * pair + c), [P, I], F32))
+                window = val2_pool[pair][:, c * X : (c + 1) * X]
                 nc.scalar.activation(second[c][:], window.indirect(col_list[:]), COPY)
-            banks = [turn(2 * u + c, second[c]) for c in range(2)]
-            for c in range(2):
-                multiply(2 * u + c, banks[c])
+            return [turn(2 * pair + c, second[c]) for c in range(2)]
+
+        turned0, turned1 = gather_and_turn(0)
+        weights = weigh_scores()
+        multiply(0, turned0, *weights)
+        multiply(1, turned1, *weights)
+        turned2, turned3 = gather_and_turn(1)
+        res = tile("res", [P, PACK, Q], F32, after="diff%d" % LAST)
+        hand_out(res, slice(0, 2), nc.sync)
+        multiply(2, turned2, *weights)
+        hand_out(res, slice(2, LAST), nc.sync)
+        multiply(LAST, turned3, *weights)
 
         res_bf = tile("res_bf", [P, Q, PACK], BF16)
-        nc.vector.tensor_copy(res_bf[:, :P, :], res_bank[0][:].rearrange("p j q -> p q j"))
-        nc.scalar.copy(res_bf[:, P:, :], res_bank[1][:].rearrange("p j q -> p q j"))
-        for h in reversed(range(HALVES)):
-            nc.scalar.copy(res[:, last, h * P : (h + 1) * P], res_bank[h][:, last, :])
-        res_words = tile("res_words", [P, Q], U32)
-        res_scale = tile("res_scale", [P, Q], U8)
-        nc.vector.quantize_mx(
-            out=res_words[:].bitcast(FP8X4), scales=res_scale[:], in_=res_bf[:].rearrange("p q j -> p (q j)")
-        )
-        nc.scalar.dma_start(out=out_v[:, last, :], in_=res[:, last, :])
-        nc.sync.dma_start(
-            out=out_1[0].rearrange("p q j -> p (q j)").bitcast(I32), in_=res_words[:].bitcast(I32)
-        )
-        for g in range(4):
+        nc.vector.tensor_copy(res_bf[:, :P, :], res_bank[0][:].rearrange("p t q -> p q t"))
+        nc.scalar.copy(res_bf[:, P:, :], res_bank[1][:].rearrange("p t q -> p q t"))
+        hand_out(res, slice(LAST, PACK), nc.scalar)
+        res_words, res_scale = quantise("res", res_bf[:].rearrange("p q t -> p (q t)"), Q)
+        nc.sync.dma_start(out=out_1[0].rearrange("p q t -> p (q t)").bitcast(I32), in_=res_words[:].bitcast(I32))
+        for g in range(QUADRANTS):
             queue = nc.sync if g % 2 == 0 else nc.scalar
             queue.dma_start(
-                out=out_2[0, 4 * g : 4 * g + 4, :].bitcast(I32), in_=res_scale[32 * g : 32 * g + 4, :].bitcast(I32)
+                out=out_2[0, SCALE_ROWS * g : SCALE_ROWS * (g + 1), :].bitcast(I32),
+                in_=scale_rows(res_scale, g).bitcast(I32),
             )

from contextlib import ExitStack

import concourse.mybir as mybir
from concourse.masks import make_identity

D, T, I, Q, E, U, X = 512, 2048, 512, 256, 512, 1024, 1024
FLOPS = 2 * (2 * D * Q * I + I * E * Q)

F32 = mybir.dt.float32
BF16 = mybir.dt.bfloat16
I32 = mybir.dt.int32
U32 = mybir.dt.uint32
U16 = mybir.dt.uint16
U8 = mybir.dt.uint8
FP8X4 = mybir.dt.float8_e4m3fn_x4
FP4X4 = mybir.dt.float4_e2m1fn_x4
COPY = mybir.ActivationFunctionType.Copy
ABS = mybir.ActivationFunctionType.Abs
MULT = mybir.AluOpType.mult
SUB = mybir.AluOpType.subtract

P = 128
PACK = 4
LAST = PACK - 1
HALVES = Q // P
GROUP = 16
QUADRANTS, QUADRANT = 4, 32
SCALE_ROWS = 4
BLOCK_PARTITIONS = 8
LINE_F32, LINE_WORDS = 4, 2
TAIL_PIECES = 2


def tile_attend_twosources_apartvalues_lean_pl_kernel(
    tc, query, query2, keys_words, keys_scales, notes, wfac, vals, vals2, vfac, offs, offs2, offs3, out_0, out_1, out_2
):
    nc = tc.nc
    with ExitStack() as ctx:
        sb = ctx.enter_context(tc.tile_pool(name="sb", bufs=1))
        ps = ctx.enter_context(tc.psum_pool(name="ps", bufs=1))
        ps_turned = ctx.enter_context(tc.psum_pool(name="ps_turned", bufs=2))

        def tile(name, shape, dtype, after=None):
            return sb.tile(shape, dtype, name=name, tag=after or name, align_bytes=64)

        def planes(name, width):
            return [tile("%s%d" % (name, t), [P, width], F32) for t in range(PACK)]

        def by_plane(rows):
            return rows.rearrange("(p t) c -> p t c", t=PACK)

        def by_slot(factors):
            return factors.rearrange("o (s r) -> (o s) r", r=PACK)

        def scale_rows(scales, g):
            return scales[QUADRANT * g : QUADRANT * g + SCALE_ROWS]

        tok_list = tile("tok_list", [P, I // GROUP], U16)
        note_list = tile("note_list", [P, I // GROUP], U16)
        col_list = tile("col_list", [P, I // GROUP], U16)
        key_pool = tile("key_pool", [P, T], U16)
        key_scale_pool = tile("key_scale_pool", [P, T], U8)
        note_pool = planes("note_pool", U)
        val_pool = planes("val_pool", T)
        val2_pool = [tile("val2_pool%d" % u, [P, 2 * X], F32) for u in range(2)]
        q_raw = [tile("q_raw%d" % a, [P, PACK, Q], F32) for a in range(2)]
        wfac_sb = tile("wfac_sb", [P, PACK], F32)
        vfac_sb = tile("vfac_sb", [P, PACK], F32)
        ident = tile("ident", [P, P], F32)

        nc.gpsimd.memset(key_scale_pool[:].bitcast(I32), 0)
        make_identity(nc, ident[:])

        nc.sync.dma_start(key_pool[:].bitcast(I32), keys_words[0].bitcast(I32))
        nc.sync.dma_start(tok_list[:], offs)
        nc.sync.dma_start(key_scale_pool[0:P:BLOCK_PARTITIONS, :].bitcast(I32), keys_scales[0].bitcast(I32))
        nc.sync.dma_start(note_pool[0][:], by_plane(notes)[:, 0, :])
        nc.sync.dma_start(note_list[:], offs2)
        nc.sync.dma_start(note_pool[1][:], by_plane(notes)[:, 1, :])
        nc.sync.dma_start(q_raw[0][:], by_plane(query))
        nc.sync.dma_start(note_pool[2][:], by_plane(notes)[:, 2, :])
        nc.sync.dma_start(note_pool[3][:], by_plane(notes)[:, 3, :])
        nc.sync.dma_start(q_raw[1][:], by_plane(query2))

        key_listed = tile("key_listed", [P, I], U16)
        key_words = tile("key_words", [P, PACK, P], U16)
        key_scale = tile("key_scale", [P, PACK, P], U8)
        nc.vector.tensor_copy(key_listed[:], key_pool[:].indirect(tok_list[:]))
        nc.vector.tensor_copy(key_words[:], key_listed[:].rearrange("p (s r) -> p r s", r=PACK))
        key_scale_listed = tile("key_scale_listed", [P, PACK, P], U8)
        nc.vector.tensor_copy(key_scale_listed[:].rearrange("p r s -> p s r"), key_scale_pool[:].indirect(tok_list[:]))
        nc.gpsimd.memset(key_scale[:].rearrange("p r s -> p (r s)").bitcast(I32), 0)
        for g in range(QUADRANTS):
            spread = key_scale_listed[QUADRANT * g : QUADRANT * (g + 1) : BLOCK_PARTITIONS]
            nc.sync.dma_start(
                scale_rows(key_scale, g).rearrange("p r s -> p (r s)").bitcast(I32),
                spread.rearrange("p r s -> p (r s)").bitcast(I32),
            )

        nc.sync.dma_start(wfac_sb[:], by_slot(wfac))
        for t in range(PACK):
            if t % 2 == 0:
                nc.sync.dma_start(val2_pool[t // 2][:], by_plane(vals2)[:, t : t + 2, :].rearrange("p t x -> p (t x)"))
            if t == 0:
                nc.sync.dma_start(col_list[:], offs3)
                nc.sync.dma_start(vfac_sb[:], by_slot(vfac))
            nc.sync.dma_start(val_pool[t][:], by_plane(vals)[:, t, :])

        def quantise(name, values, width, after=None):
            words = tile(name + "_words", [P, width], U32, after=after)
            scale = tile(name + "_scale", [P, width], U8)
            nc.vector.quantize_mx(out=words[:].bitcast(FP8X4), scales=scale[:], in_=values)
            return words, scale

        def weave_queries(a, copy):
            q_bf = tile("q_bf%d" % a, [P, Q, PACK], BF16)
            copy(
                q_bf[:].rearrange("p (c n) t -> p c t n", n=LINE_F32),
                q_raw[a][:].rearrange("p t (c n) -> p c t n", n=LINE_F32),
            )
            return q_bf[:].rearrange("p q t -> p (q t)")

        def factor(factors):
            return factors[:].unsqueeze(1).to_broadcast([P, P, PACK])

        q_key_words, q_key_scale = quantise("q_key", weave_queries(0, nc.vector.tensor_copy), Q)
        note_listed = tile("note_listed", [P, PACK, I], BF16)
        for t in range(PACK):
            nc.scalar.activation(note_listed[:, t, :], note_pool[t][:].indirect(note_list[:]), COPY)
        q_note_bf = weave_queries(1, nc.scalar.copy)
        note_bf = tile("note_bf", [P, PACK, P, PACK], BF16)
        nc.vector.tensor_copy(
            note_bf[:].rearrange("p r (c n) t -> p r c t n", n=LINE_WORDS),
            note_listed[:].rearrange("p t (c n r) -> p r c t n", n=LINE_WORDS, r=PACK),
        )
        q_note_words, q_note_scale = quantise("q_note", q_note_bf, Q)
        note_words, note_scale = quantise("note", note_bf[:].rearrange("p r s t -> p (r s t)"), I)

        score = [ps.tile([P, PACK, P], F32, name="score%d" % h) for h in range(HALVES)]
        for h in range(HALVES):
            rows = slice(h * P, (h + 1) * P)
            for r in range(PACK):
                nc.tensor.matmul_mx(
                    out=score[h][:, r, :],
                    lhsT=key_words[:, r, :].bitcast(FP4X4),
                    lhsT_scale=key_scale[:, r, :],
                    rhs=q_key_words[:, rows].bitcast(FP8X4),
                    rhs_scale=q_key_scale[:, rows],
                    start=(r == 0),
                    stop=False,
                )
        for h in range(HALVES):
            rows = slice(h * P, (h + 1) * P)
            for r in range(PACK):
                nc.tensor.matmul_mx(
                    out=score[h][:, r, :],
                    lhsT=note_words[:, r * P : (r + 1) * P].bitcast(FP8X4),
                    lhsT_scale=note_scale[:, r * P : (r + 1) * P],
                    rhs=q_note_words[:, rows].bitcast(FP8X4),
                    rhs_scale=q_note_scale[:, rows],
                    start=False,
                    stop=(r == LAST),
                )

        res_bank = [ps.tile([P, PACK, P], F32, name="res_bank%d" % h) for h in range(HALVES)]

        def turn(t, second):
            diff = tile("diff%d" % t, [P, I], F32)
            dist = tile("dist%d" % t, [P, PACK, P], F32)
            pieces = TAIL_PIECES if t == LAST else 1
            n = I // pieces
            for c in range(pieces):
                slots = slice(c * n, (c + 1) * n)
                listed = val_pool[t][:].indirect(tok_list[:, c * n // GROUP : (c + 1) * n // GROUP])
                nc.vector.tensor_tensor(diff[:, slots], listed, second[:, slots], SUB)
                nc.scalar.activation(
                    dist[:, :, c * n // PACK : (c + 1) * n // PACK].rearrange("p r s -> p s r"),
                    diff[:, slots].rearrange("p (s r) -> p s r", r=PACK),
                    ABS,
                )
            turned = ps_turned.tile([P, PACK, P], F32, name="turned")
            for r in range(PACK):
                nc.tensor.transpose(turned[:, r, :], dist[:, r, :], ident[:])
            return turned

        def weigh_scores():
            w_bf = tile("w_bf", [P, Q, PACK], BF16, after="second0")
            for h in range(HALVES):
                nc.vector.tensor_tensor(
                    w_bf[:, h * P : (h + 1) * P, :], score[h][:].rearrange("s r q -> s q r"), factor(wfac_sb), MULT
                )
            return quantise("w", w_bf[:].rearrange("s q r -> s (q r)"), Q, after="val_pool1")

        def multiply(t, turned, w_words, w_scale):
            v_bf = tile("v_bf%d" % t, [P, P, PACK], BF16, after="second%d" % (t + 1) if t % 2 == 0 else None)
            nc.vector.tensor_tensor(v_bf[:], turned[:].rearrange("s r p -> s p r"), factor(vfac_sb), MULT)
            v_words, v_scale = quantise("v%d" % t, v_bf[:].rearrange("s p r -> s (p r)"), P)
            for h in range(HALVES):
                nc.tensor.matmul_mx(
                    out=res_bank[h][:, t, :],
                    lhsT=v_words[:].bitcast(FP8X4),
                    lhsT_scale=v_scale[:],
                    rhs=w_words[:, h * P : (h + 1) * P].bitcast(FP8X4),
                    rhs_scale=w_scale[:, h * P : (h + 1) * P],
                    start=True,
                    stop=True,
                )

        def hand_out(res, done, queue):
            for h in reversed(range(HALVES)):
                nc.scalar.copy(res[:, done, h * P : (h + 1) * P], res_bank[h][:, done, :])
            queue.dma_start(out=by_plane(out_0)[:, done, :], in_=res[:, done, :])

        def gather_and_turn(pair):
            second = []
            for c in range(2):
                second.append(tile("second%d" % (2 * pair + c), [P, I], F32))
                window = val2_pool[pair][:, c * X : (c + 1) * X]
                nc.scalar.activation(second[c][:], window.indirect(col_list[:]), COPY)
            return [turn(2 * pair + c, second[c]) for c in range(2)]

        turned0, turned1 = gather_and_turn(0)
        weights = weigh_scores()
        multiply(0, turned0, *weights)
        multiply(1, turned1, *weights)
        turned2, turned3 = gather_and_turn(1)
        res = tile("res", [P, PACK, Q], F32, after="diff%d" % LAST)
        hand_out(res, slice(0, 2), nc.sync)
        multiply(2, turned2, *weights)
        hand_out(res, slice(2, LAST), nc.sync)
        multiply(LAST, turned3, *weights)

        res_bf = tile("res_bf", [P, Q, PACK], BF16)
        nc.vector.tensor_copy(res_bf[:, :P, :], res_bank[0][:].rearrange("p t q -> p q t"))
        nc.scalar.copy(res_bf[:, P:, :], res_bank[1][:].rearrange("p t q -> p q t"))
        hand_out(res, slice(LAST, PACK), nc.scalar)
        res_words, res_scale = quantise("res", res_bf[:].rearrange("p q t -> p (q t)"), Q)
        nc.sync.dma_start(out=out_1[0].rearrange("p q t -> p (q t)").bitcast(I32), in_=res_words[:].bitcast(I32))
        for g in range(QUADRANTS):
            queue = nc.sync if g % 2 == 0 else nc.scalar
            queue.dma_start(
                out=out_2[0, SCALE_ROWS * g : SCALE_ROWS * (g + 1), :].bitcast(I32),
                in_=scale_rows(res_scale, g).bitcast(I32),
            )
